import numpy as np
import ml_dtypes


def mxq(x, axis, fmt="e4m3"):
    dtype, down = {"e4m3": (ml_dtypes.float8_e4m3fn, 7), "e5m2": (ml_dtypes.float8_e5m2, 14)}[fmt]
    v = np.moveaxis(np.asarray(x, np.float32).astype(ml_dtypes.bfloat16).astype(np.float64), axis, -1)
    blocks = v.reshape(v.shape[:-1] + (-1, 32))
    amax = np.abs(blocks).max(-1, keepdims=True)
    byte = np.maximum(np.where(amax > 0, np.frexp(amax)[1] - 1 + 127, 0) - down, 1)
    scale = np.exp2(byte - 127.0)
    codes = (blocks / scale).astype(np.float32).astype(dtype).astype(np.float64)
    return np.moveaxis((codes * scale).reshape(v.shape), -1, axis)


WIDE = False


def mx_kscale(k):
    if not WIDE:
        return np.ones(k)
    levels = np.array([10, -10, 5, -5, 0])
    if k % 512:
        return np.exp2(np.random.permutation(np.resize(levels, k // 32))).repeat(32)
    a = np.empty((k // 512, 16))
    for p in range(k // 512):
        a[p, :8] = np.random.permutation(np.resize(levels, 8))
        for g in range(8):
            far = levels[np.abs(levels - a[p, g]) >= 10]
            a[p, g + 8] = far[np.random.randint(len(far))]
    return np.exp2(a.ravel()).repeat(32)


def f64(x):
    return np.asarray(x).astype(np.float64)


def striped8(idx):
    return np.asarray(idx).reshape(8, -1, 16).transpose(0, 2, 1).reshape(128, -1).astype(np.uint16)


def unstriped8(offs):
    return offs.reshape(8, 16, -1).transpose(0, 2, 1).reshape(8, -1).astype(np.int64)


def pick8(x, idx, run):
    r = np.arange(len(x))
    return x[r[:, None], idx[r % (8 * run) // run]]


E2M1 = np.array([0.0, 0.5, 1.0, 1.5, 2.0, 3.0, 4.0, 6.0, -0.0, -0.5, -1.0, -1.5, -2.0, -3.0, -4.0, -6.0])


def pack_weight(w, fmt):
    k, n = w.shape
    w = f64(np.asarray(w, np.float32).astype(ml_dtypes.bfloat16)).reshape(k // 32, 32, n)
    amax = np.abs(w).max(1)
    if fmt == "e4m3":
        byte = np.frexp(amax)[1] - 1 + 127 - 7
    else:
        mant, ex = np.frexp(amax / 6.0)
        byte = np.where(mant > 0.5, ex, ex - 1) + 127
    byte = np.clip(np.where(amax > 0, byte, 1), 1, 254)
    scaled = (w * np.exp2(127.0 - byte)[:, None, :]).reshape(k, n).astype(np.float32)
    by_word = np.ascontiguousarray(scaled.reshape(k // 512, 128, 4, n).transpose(0, 1, 3, 2))
    if fmt == "e4m3":
        words = by_word.astype(ml_dtypes.float8_e4m3fn).view(np.uint8)
    else:
        c = by_word.astype(ml_dtypes.float4_e2m1fn).view(np.uint8) & 0xF
        words = (c[..., 0::2] | (c[..., 1::2] << 4)).reshape(k // 512, 128, 2 * n)
    return np.ascontiguousarray(words), np.ascontiguousarray(byte.astype(np.uint8).reshape(k // 512, 16, n))


def unpack_weight(words, scales, fmt):
    g, _, n = scales.shape
    words = np.ascontiguousarray(words).reshape(g, 128, n, -1)
    if fmt == "e4m3":
        vals = words.view(ml_dtypes.float8_e4m3fn).astype(np.float64)
    else:
        nib = np.empty((g, 128, n, 4), np.uint8)
        nib[..., 0::2] = words & 0xF
        nib[..., 1::2] = words >> 4
        vals = E2M1[nib]
    vals = vals * np.repeat(np.exp2(scales.astype(np.float64) - 127.0), 8, axis=1)[..., None]
    return vals.transpose(0, 1, 3, 2).reshape(g * 512, n)


D, T, I, Q = 512, 1024, 512, 128


def setup_inputs():
    n = np.random.standard_normal
    idx = np.stack([np.random.permutation(T)[:I] for _ in range(8)])
    idx2 = np.stack([np.random.permutation(T)[:I] for _ in range(8)])
    idx3 = np.stack([np.random.permutation(T)[:I] for _ in range(8)])
    fd = mx_kscale(D)
    keysp = pack_weight(n((D, T)) / fd[:, None], "e2m1")
    return {
        "query": (n((D, Q)) * 0.9 / np.sqrt(D) * fd[:, None]).astype(np.float32),
        "query2": (n((D, Q)) * 0.9 / np.sqrt(D) * fd[:, None]).astype(np.float32),
        "keys_words": keysp[0],
        "keys_scales": keysp[1],
        "lam": (np.random.uniform(0.5, 1.3, (Q, 1))).astype(np.float32),
        "old": (1.0 * n((Q, T))).astype(np.float32),
        "offs": striped8(idx),
        "offs2": striped8(idx2),
        "offs3": striped8(idx3),
    }


def reference(query, query2, keys_words, keys_scales, lam, old, offs, offs2, offs3):
    idx = unstriped8(offs)
    idx2 = unstriped8(offs2)
    idx3 = unstriped8(offs3)
    keysu = unpack_weight(keys_words, keys_scales, "e2m1")
    queryq = mxq(f64(query), 0, "e4m3")
    a = queryq.T @ keysu
    query2q = mxq(f64(query2), 0, "e4m3")
    b = query2q.T @ keysu
    w = (np.maximum(pick8(a, idx, 16), pick8(b, idx2, 16)) - np.maximum(pick8(a, idx2, 16), pick8(b, idx, 16))) * f64(lam)
    f1 = np.zeros((Q, T))
    f1[np.arange(Q)[:, None], idx3[np.arange(Q) % 128 // 16]] = w
    y = np.maximum(f1, f64(old)) + f64(old) * 0.25
    return y

@@ -1,0 +1,139 @@
+from contextlib import ExitStack
+
+import concourse.mybir as mybir
+
+D, T, SLOTS, Q = 512, 1024, 512, 128
+FLOPS = 2 * 2 * D * Q * T
+
+F32 = mybir.dt.float32
+BF16 = mybir.dt.bfloat16
+I32 = mybir.dt.int32
+U32 = mybir.dt.uint32
+U16 = mybir.dt.uint16
+U8 = mybir.dt.uint8
+FP8X4 = mybir.dt.float8_e4m3fn_x4
+FP4X4 = mybir.dt.float4_e2m1fn_x4
+ALU = mybir.AluOpType
+COPY = mybir.ActivationFunctionType.Copy
+
+P = 128
+PACK = 4
+N_PASS = 256
+HALF = SLOTS // 2
+LIST_ROWS = 16
+OUT_WIDTHS = (384, 320, 192, 128)
+
+
+def tile_attend_exchanged_lean_largerput_heads_kernel(
+    tc, query, query2, keys_words, keys_scales, lam, old, offs, offs2, offs3, out
+):
+    nc = tc.nc
+    with ExitStack() as ctx:
+        lists = ctx.enter_context(tc.tile_pool(name="lists", bufs=1))
+        keep = ctx.enter_context(tc.tile_pool(name="keep", bufs=1))
+        psum = ctx.enter_context(tc.psum_pool(name="psum", bufs=1))
+
+        key_scales = keep.tile([P, T], U8, name="key_scales", align_bytes=64)
+        nc.vector.memset(key_scales[:].bitcast(U32), 0)
+
+        raw = [keep.tile([P, PACK, Q], F32, name="raw%d" % j) for j in range(2)]
+        nc.sync.dma_start(out=raw[0][:], in_=query.rearrange("(p j) w -> p j w", j=PACK))
+        for quad in range(4):
+            nc.sync.dma_start(
+                out=key_scales[32 * quad : 32 * quad + 4, :].bitcast(I32),
+                in_=keys_scales[0, 4 * quad : 4 * quad + 4, :].bitcast(I32),
+            )
+        key_words = [keep.tile([P, T], U8, name="key_words%d" % u, align_bytes=64) for u in range(2)]
+        nc.sync.dma_start(out=key_words[0][:].bitcast(I32), in_=keys_words[0, :, :T].bitcast(I32))
+        nc.sync.dma_start(out=raw[1][:], in_=query2.rearrange("(p j) w -> p j w", j=PACK))
+        nc.sync.dma_start(out=key_words[1][:].bitcast(I32), in_=keys_words[0, :, T:].bitcast(I32))
+        first = lists.tile([P, SLOTS // LIST_ROWS], U16, name="first")
+        nc.sync.dma_start(first[:], offs)
+        second = lists.tile([P, SLOTS // LIST_ROWS], U16, name="second")
+        nc.sync.dma_start(second[:], offs2)
+        lam_col = keep.tile([P, 1], F32, name="lam_col")
+        nc.sync.dma_start(out=lam_col[:], in_=lam)
+        places = lists.tile([P, SLOTS // LIST_ROWS], U16, name="places")
+        nc.sync.dma_start(places[:], offs3)
+        old_sb = keep.tile([P, T], F32, name="old_sb")
+        nc.sync.dma_start(out=old_sb[:], in_=old)
+
+        placed = keep.tile([P, T], F32, name="placed")
+        nc.vector.memset(placed[:], 0.0)
+        lam_wide = keep.tile([P, HALF], F32, name="lam_wide")
+        nc.gpsimd.tensor_scalar(lam_wide[:], lam_col[:].to_broadcast([P, HALF]), 1.0, 0.0, ALU.mult, ALU.add)
+
+        codes, scales = [], []
+        for j in range(2):
+            grouped = keep.tile([P, Q, PACK], BF16, name="grouped%d" % j, align_bytes=64)
+            nc.vector.tensor_copy(
+                out=grouped[:].rearrange("p (c i) t -> p c t i", i=4),
+                in_=raw[j][:].rearrange("p t (c i) -> p c t i", i=4),
+            )
+            codes.append(keep.tile([P, Q], U32, name="codes%d" % j, align_bytes=64))
+            scales.append(keep.tile([P, Q], U8, name="scales%d" % j, align_bytes=64))
+            nc.vector.quantize_mx(
+                out=codes[j][:].bitcast(FP8X4),
+                scales=scales[j][:],
+                in_=grouped[:].rearrange("p w j -> p (w j)"),
+            )
+
+        scores = [keep.tile([P, T], F32, name="scores%d" % j) for j in range(2)]
+        for j in range(2):
+            for n0 in range(0, T, N_PASS):
+                bank = psum.tile([P, N_PASS], F32, name="bank%d_%d" % (j, n0))
+                nc.tensor.matmul_mx(
+                    out=bank[:],
+                    lhsT=codes[j][:].bitcast(FP8X4),
+                    lhsT_scale=scales[j][:],
+                    rhs=key_words[2 * n0 // T][:, 2 * n0 % T : 2 * n0 % T + 2 * N_PASS].bitcast(FP4X4),
+                    rhs_scale=key_scales[:, n0 : n0 + N_PASS],
+                    start=True,
+                    stop=True,
+                )
+                if j == 0 and n0 + N_PASS == T:
+                    nc.vector.tensor_copy(out=scores[j][:, n0 : n0 + N_PASS], in_=bank[:])
+                else:
+                    nc.scalar.copy(scores[j][:, n0 : n0 + N_PASS], bank[:])
+        a, b = scores
+
+        from_a = keep.tile([P, 2, HALF], F32, name="from_a")
+        for h in range(2):
+            cols = slice(h * HALF // LIST_ROWS, (h + 1) * HALF // LIST_ROWS)
+            from_b = keep.tile([P, 2, HALF], F32, name="from_b%d" % h)
+            if h == 0:
+                nc.vector.tensor_copy(from_a[:, 0, :], a[:].indirect(first[:, cols]))
+                nc.vector.tensor_copy(from_a[:, 1, :], a[:].indirect(second[:, cols]))
+                nc.vector.tensor_copy(from_b[:, 0, :], b[:].indirect(second[:, cols]))
+                nc.scalar.activation(from_b[:, 1, :], b[:].indirect(first[:, cols]), COPY)
+            else:
+                nc.scalar.activation(from_b[:, 0, :], b[:].indirect(second[:, cols]), COPY)
+                nc.scalar.activation(from_b[:, 1, :], b[:].indirect(first[:, cols]), COPY)
+                nc.scalar.activation(from_a[:, 0, :], a[:].indirect(first[:, cols]), COPY)
+                nc.scalar.activation(from_a[:, 1, :], a[:].indirect(second[:, cols]), COPY)
+            larger = keep.tile([P, 2, HALF], F32, name="larger%d" % h)
+            diff = keep.tile([P, HALF], F32, name="diff%d" % h)
+            pieces = (slice(0, HALF // 2), slice(HALF // 2, HALF))
+            for piece in pieces:
+                nc.vector.tensor_tensor(larger[:, :, piece], from_a[:, :, piece], from_b[:, :, piece], ALU.max)
+            for piece in pieces:
+                nc.vector.tensor_tensor(diff[:, piece], larger[:, 0, piece], larger[:, 1, piece], ALU.subtract)
+            nc.vector.tensor_tensor(placed[:].indirect(places[:, cols]), diff[:], lam_wide[:], ALU.mult)
+
+        pending = None
+        c0 = 0
+        for width in OUT_WIDTHS:
+            cols = slice(c0, c0 + width)
+            top = keep.tile([P, width], F32, name="top%d" % c0)
+            nc.vector.tensor_tensor(top[:], placed[:, cols], old_sb[:, cols], ALU.max)
+            if pending is not None:
+                finish(nc, keep, old_sb, out, *pending)
+            pending = (top, cols)
+            c0 = c0 + width
+        finish(nc, keep, old_sb, out, *pending)
+
+
+def finish(nc, keep, old_sb, out, top, cols):
+    result = keep.tile([P, cols.stop - cols.start], F32, name="result%d" % cols.start)
+    nc.vector.scalar_tensor_tensor(result[:], old_sb[:, cols], 0.25, top[:], ALU.mult, ALU.add)
+    nc.sync.dma_start(out=out[:, cols], in_=result[:])

@@ -18,7 +18,7 @@ COPY = mybir.ActivationFunctionType.Copy
 
 P = 128
 PACK = 4
-N_PASS = 256
+PASSES = ((0, 256), (256, 256), (512, 256), (768, 128), (896, 128))
 HALF = SLOTS // 2
 LIST_ROWS = 16
 OUT_WIDTHS = (384, 320, 192, 128)
@@ -38,13 +38,14 @@ def tile_attend_exchanged_lean_largerput_heads_kernel(
 
         raw = [keep.tile([P, PACK, Q], F32, name="raw%d" % j) for j in range(2)]
         nc.sync.dma_start(out=raw[0][:], in_=query.rearrange("(p j) w -> p j w", j=PACK))
+        key_words = [keep.tile([P, T], U8, name="key_words%d" % u, align_bytes=64) for u in range(2)]
+        nc.sync.dma_start(out=key_words[0][:].bitcast(I32), in_=keys_words[0, :, :T].bitcast(I32))
         for quad in range(4):
-            nc.sync.dma_start(
+            queue = nc.scalar if quad < 2 else nc.sync
+            queue.dma_start(
                 out=key_scales[32 * quad : 32 * quad + 4, :].bitcast(I32),
                 in_=keys_scales[0, 4 * quad : 4 * quad + 4, :].bitcast(I32),
             )
-        key_words = [keep.tile([P, T], U8, name="key_words%d" % u, align_bytes=64) for u in range(2)]
-        nc.sync.dma_start(out=key_words[0][:].bitcast(I32), in_=keys_words[0, :, :T].bitcast(I32))
         nc.sync.dma_start(out=raw[1][:], in_=query2.rearrange("(p j) w -> p j w", j=PACK))
         nc.sync.dma_start(out=key_words[1][:].bitcast(I32), in_=keys_words[0, :, T:].bitcast(I32))
         first = lists.tile([P, SLOTS // LIST_ROWS], U16, name="first")
@@ -65,36 +66,39 @@ def tile_attend_exchanged_lean_largerput_heads_kernel(
 
         codes, scales = [], []
         for j in range(2):
-            grouped = keep.tile([P, Q, PACK], BF16, name="grouped%d" % j, align_bytes=64)
-            nc.vector.tensor_copy(
-                out=grouped[:].rearrange("p (c i) t -> p c t i", i=4),
-                in_=raw[j][:].rearrange("p t (c i) -> p c t i", i=4),
-            )
+            grouped = keep.tile([P, Q, PACK], BF16, name="grouped%d" % j, tag="grouped", align_bytes=64)
             codes.append(keep.tile([P, Q], U32, name="codes%d" % j, align_bytes=64))
             scales.append(keep.tile([P, Q], U8, name="scales%d" % j, align_bytes=64))
-            nc.vector.quantize_mx(
-                out=codes[j][:].bitcast(FP8X4),
-                scales=scales[j][:],
-                in_=grouped[:].rearrange("p w j -> p (w j)"),
-            )
+            halves = (slice(0, Q // 2), slice(Q // 2, Q))
+            for rows in halves:
+                nc.vector.tensor_copy(
+                    out=grouped[:, rows, :].rearrange("p (c i) t -> p c t i", i=4),
+                    in_=raw[j][:, :, rows].rearrange("p t (c i) -> p c t i", i=4),
+                )
+            for rows in halves:
+                nc.vector.quantize_mx(
+                    out=codes[j][:, rows].bitcast(FP8X4),
+                    scales=scales[j][:, rows],
+                    in_=grouped[:, rows, :].rearrange("p w j -> p (w j)"),
+                )
 
         scores = [keep.tile([P, T], F32, name="scores%d" % j) for j in range(2)]
-        for j in range(2):
-            for n0 in range(0, T, N_PASS):
-                bank = psum.tile([P, N_PASS], F32, name="bank%d_%d" % (j, n0))
-                nc.tensor.matmul_mx(
-                    out=bank[:],
-                    lhsT=codes[j][:].bitcast(FP8X4),
-                    lhsT_scale=scales[j][:],
-                    rhs=key_words[2 * n0 // T][:, 2 * n0 % T : 2 * n0 % T + 2 * N_PASS].bitcast(FP4X4),
-                    rhs_scale=key_scales[:, n0 : n0 + N_PASS],
-                    start=True,
-                    stop=True,
-                )
-                if j == 0 and n0 + N_PASS == T:
-                    nc.vector.tensor_copy(out=scores[j][:, n0 : n0 + N_PASS], in_=bank[:])
-                else:
-                    nc.scalar.copy(scores[j][:, n0 : n0 + N_PASS], bank[:])
+        passes = [(j, n0, width) for j in range(2) for n0, width in PASSES]
+        for k, (j, n0, width) in enumerate(passes):
+            bank = psum.tile([P, width], F32, name="bank%d_%d" % (j, n0), tag="bank%d" % (k % 8))
+            nc.tensor.matmul_mx(
+                out=bank[:],
+                lhsT=codes[j][:].bitcast(FP8X4),
+                lhsT_scale=scales[j][:],
+                rhs=key_words[2 * n0 // T][:, 2 * n0 % T : 2 * n0 % T + 2 * width].bitcast(FP4X4),
+                rhs_scale=key_scales[:, n0 : n0 + width],
+                start=True,
+                stop=True,
+            )
+            if j == 0 and n0 + width == T:
+                nc.vector.tensor_copy(out=scores[j][:, n0 : n0 + width], in_=bank[:])
+            else:
+                nc.scalar.copy(scores[j][:, n0 : n0 + width], bank[:])
         a, b = scores
 
         from_a = keep.tile([P, 2, HALF], F32, name="from_a")

@@ -18,9 +18,13 @@ COPY = mybir.ActivationFunctionType.Copy
 
 P = 128
 PACK = 4
-PASSES = ((0, 256), (256, 256), (512, 256), (768, 128), (896, 128))
+QUADRANT = 32
+SCALE_ROWS = 4
+BANKS = 8
+HEAD_ROWS = 16
 HALF = SLOTS // 2
-LIST_ROWS = 16
+RUN = 4
+PASSES = ((0, 256), (256, 256), (512, 256), (768, 128), (896, 128))
 OUT_WIDTHS = (384, 320, 192, 128)
 
 
@@ -40,29 +44,27 @@ def tile_attend_exchanged_lean_largerput_heads_kernel(
         nc.sync.dma_start(out=raw[0][:], in_=query.rearrange("(p j) w -> p j w", j=PACK))
         key_words = [keep.tile([P, T], U8, name="key_words%d" % u, align_bytes=64) for u in range(2)]
         nc.sync.dma_start(out=key_words[0][:].bitcast(I32), in_=keys_words[0, :, :T].bitcast(I32))
-        for quad in range(4):
+        for quad in range(P // QUADRANT):
             queue = nc.scalar if quad < 2 else nc.sync
             queue.dma_start(
-                out=key_scales[32 * quad : 32 * quad + 4, :].bitcast(I32),
-                in_=keys_scales[0, 4 * quad : 4 * quad + 4, :].bitcast(I32),
+                out=key_scales[QUADRANT * quad : QUADRANT * quad + SCALE_ROWS, :].bitcast(I32),
+                in_=keys_scales[0, SCALE_ROWS * quad : SCALE_ROWS * (quad + 1), :].bitcast(I32),
             )
         nc.sync.dma_start(out=raw[1][:], in_=query2.rearrange("(p j) w -> p j w", j=PACK))
         nc.sync.dma_start(out=key_words[1][:].bitcast(I32), in_=keys_words[0, :, T:].bitcast(I32))
-        first = lists.tile([P, SLOTS // LIST_ROWS], U16, name="first")
+        first = lists.tile([P, SLOTS // HEAD_ROWS], U16, name="first")
         nc.sync.dma_start(first[:], offs)
-        second = lists.tile([P, SLOTS // LIST_ROWS], U16, name="second")
+        second = lists.tile([P, SLOTS // HEAD_ROWS], U16, name="second")
         nc.sync.dma_start(second[:], offs2)
         lam_col = keep.tile([P, 1], F32, name="lam_col")
         nc.sync.dma_start(out=lam_col[:], in_=lam)
-        places = lists.tile([P, SLOTS // LIST_ROWS], U16, name="places")
+        places = lists.tile([P, SLOTS // HEAD_ROWS], U16, name="places")
         nc.sync.dma_start(places[:], offs3)
         old_sb = keep.tile([P, T], F32, name="old_sb")
         nc.sync.dma_start(out=old_sb[:], in_=old)
 
         placed = keep.tile([P, T], F32, name="placed")
         nc.vector.memset(placed[:], 0.0)
-        lam_wide = keep.tile([P, HALF], F32, name="lam_wide")
-        nc.gpsimd.tensor_scalar(lam_wide[:], lam_col[:].to_broadcast([P, HALF]), 1.0, 0.0, ALU.mult, ALU.add)
 
         codes, scales = [], []
         for j in range(2):
@@ -72,8 +74,8 @@ def tile_attend_exchanged_lean_largerput_heads_kernel(
             halves = (slice(0, Q // 2), slice(Q // 2, Q))
             for rows in halves:
                 nc.vector.tensor_copy(
-                    out=grouped[:, rows, :].rearrange("p (c i) t -> p c t i", i=4),
-                    in_=raw[j][:, :, rows].rearrange("p t (c i) -> p c t i", i=4),
+                    out=grouped[:, rows, :].rearrange("p (c i) t -> p c t i", i=RUN),
+                    in_=raw[j][:, :, rows].rearrange("p t (c i) -> p c t i", i=RUN),
                 )
             for rows in halves:
                 nc.vector.quantize_mx(
@@ -85,12 +87,13 @@ def tile_attend_exchanged_lean_largerput_heads_kernel(
         scores = [keep.tile([P, T], F32, name="scores%d" % j) for j in range(2)]
         passes = [(j, n0, width) for j in range(2) for n0, width in PASSES]
         for k, (j, n0, width) in enumerate(passes):
-            bank = psum.tile([P, width], F32, name="bank%d_%d" % (j, n0), tag="bank%d" % (k % 8))
+            bank = psum.tile([P, width], F32, name="bank%d_%d" % (j, n0), tag="bank%d" % (k % BANKS))
+            byte0 = 2 * n0
             nc.tensor.matmul_mx(
                 out=bank[:],
                 lhsT=codes[j][:].bitcast(FP8X4),
                 lhsT_scale=scales[j][:],
-                rhs=key_words[2 * n0 // T][:, 2 * n0 % T : 2 * n0 % T + 2 * width].bitcast(FP4X4),
+                rhs=key_words[byte0 // T][:, byte0 % T : byte0 % T + 2 * width].bitcast(FP4X4),
                 rhs_scale=key_scales[:, n0 : n0 + width],
                 start=True,
                 stop=True,
@@ -101,9 +104,9 @@ def tile_attend_exchanged_lean_largerput_heads_kernel(
                 nc.scalar.copy(scores[j][:, n0 : n0 + width], bank[:])
         a, b = scores
 
-        from_a = keep.tile([P, 2, HALF], F32, name="from_a")
         for h in range(2):
-            cols = slice(h * HALF // LIST_ROWS, (h + 1) * HALF // LIST_ROWS)
+            cols = slice(h * HALF // HEAD_ROWS, (h + 1) * HALF // HEAD_ROWS)
+            from_a = keep.tile([P, 2, HALF], F32, name="from_a%d" % h, tag="pair%d" % h)
             from_b = keep.tile([P, 2, HALF], F32, name="from_b%d" % h)
             if h == 0:
                 nc.vector.tensor_copy(from_a[:, 0, :], a[:].indirect(first[:, cols]))
@@ -115,14 +118,13 @@ def tile_attend_exchanged_lean_largerput_heads_kernel(
                 nc.scalar.activation(from_b[:, 1, :], b[:].indirect(first[:, cols]), COPY)
                 nc.scalar.activation(from_a[:, 0, :], a[:].indirect(first[:, cols]), COPY)
                 nc.scalar.activation(from_a[:, 1, :], a[:].indirect(second[:, cols]), COPY)
-            larger = keep.tile([P, 2, HALF], F32, name="larger%d" % h)
-            diff = keep.tile([P, HALF], F32, name="diff%d" % h)
-            pieces = (slice(0, HALF // 2), slice(HALF // 2, HALF))
-            for piece in pieces:
-                nc.vector.tensor_tensor(larger[:, :, piece], from_a[:, :, piece], from_b[:, :, piece], ALU.max)
-            for piece in pieces:
-                nc.vector.tensor_tensor(diff[:, piece], larger[:, 0, piece], larger[:, 1, piece], ALU.subtract)
-            nc.vector.tensor_tensor(placed[:].indirect(places[:, cols]), diff[:], lam_wide[:], ALU.mult)
+            larger = keep.tile([P, 2, HALF], F32, name="larger%d" % h, tag="pair%d" % (h + 1))
+            scaled = keep.tile([P, 2, HALF], F32, name="scaled%d" % h)
+            for side in range(2):
+                nc.vector.tensor_tensor(larger[:, side, :], from_a[:, side, :], from_b[:, side, :], ALU.max)
+            for side, sign in enumerate((1.0, -1.0)):
+                nc.vector.tensor_scalar(scaled[:, side, :], larger[:, side, :], lam_col[:], sign, ALU.mult, ALU.mult)
+            nc.vector.tensor_tensor(placed[:].indirect(places[:, cols]), scaled[:, 0, :], scaled[:, 1, :], ALU.add)
 
         pending = None
         c0 = 0
@@ -131,13 +133,13 @@ def tile_attend_exchanged_lean_largerput_heads_kernel(
             top = keep.tile([P, width], F32, name="top%d" % c0)
             nc.vector.tensor_tensor(top[:], placed[:, cols], old_sb[:, cols], ALU.max)
             if pending is not None:
-                finish(nc, keep, old_sb, out, *pending)
+                add_and_store(nc, keep, old_sb, out, *pending)
             pending = (top, cols)
             c0 = c0 + width
-        finish(nc, keep, old_sb, out, *pending)
+        add_and_store(nc, keep, old_sb, out, *pending)
 
 
-def finish(nc, keep, old_sb, out, top, cols):
+def add_and_store(nc, keep, old_sb, out, top, cols):
     result = keep.tile([P, cols.stop - cols.start], F32, name="result%d" % cols.start)
     nc.vector.scalar_tensor_tensor(result[:], old_sb[:, cols], 0.25, top[:], ALU.mult, ALU.add)
     nc.sync.dma_start(out=out[:, cols], in_=result[:])

from contextlib import ExitStack

import concourse.mybir as mybir

D, T, SLOTS, Q = 512, 1024, 512, 128
FLOPS = 2 * 2 * D * Q * T

F32 = mybir.dt.float32
BF16 = mybir.dt.bfloat16
I32 = mybir.dt.int32
U32 = mybir.dt.uint32
U16 = mybir.dt.uint16
U8 = mybir.dt.uint8
FP8X4 = mybir.dt.float8_e4m3fn_x4
FP4X4 = mybir.dt.float4_e2m1fn_x4
ALU = mybir.AluOpType
COPY = mybir.ActivationFunctionType.Copy

P = 128
PACK = 4
QUADRANT = 32
SCALE_ROWS = 4
BANKS = 8
HEAD_ROWS = 16
HALF = SLOTS // 2
RUN = 4
PASSES = ((0, 256), (256, 256), (512, 256), (768, 128), (896, 128))
OUT_WIDTHS = (384, 320, 192, 128)


def tile_attend_exchanged_lean_largerput_heads_kernel(
    tc, query, query2, keys_words, keys_scales, lam, old, offs, offs2, offs3, out
):
    nc = tc.nc
    with ExitStack() as ctx:
        lists = ctx.enter_context(tc.tile_pool(name="lists", bufs=1))
        keep = ctx.enter_context(tc.tile_pool(name="keep", bufs=1))
        psum = ctx.enter_context(tc.psum_pool(name="psum", bufs=1))

        key_scales = keep.tile([P, T], U8, name="key_scales", align_bytes=64)
        nc.vector.memset(key_scales[:].bitcast(U32), 0)

        raw = [keep.tile([P, PACK, Q], F32, name="raw%d" % j) for j in range(2)]
        nc.sync.dma_start(out=raw[0][:], in_=query.rearrange("(p j) w -> p j w", j=PACK))
        key_words = [keep.tile([P, T], U8, name="key_words%d" % u, align_bytes=64) for u in range(2)]
        nc.sync.dma_start(out=key_words[0][:].bitcast(I32), in_=keys_words[0, :, :T].bitcast(I32))
        for quad in range(P // QUADRANT):
            queue = nc.scalar if quad < 2 else nc.sync
            queue.dma_start(
                out=key_scales[QUADRANT * quad : QUADRANT * quad + SCALE_ROWS, :].bitcast(I32),
                in_=keys_scales[0, SCALE_ROWS * quad : SCALE_ROWS * (quad + 1), :].bitcast(I32),
            )
        nc.sync.dma_start(out=raw[1][:], in_=query2.rearrange("(p j) w -> p j w", j=PACK))
        nc.sync.dma_start(out=key_words[1][:].bitcast(I32), in_=keys_words[0, :, T:].bitcast(I32))
        first = lists.tile([P, SLOTS // HEAD_ROWS], U16, name="first")
        nc.sync.dma_start(first[:], offs)
        second = lists.tile([P, SLOTS // HEAD_ROWS], U16, name="second")
        nc.sync.dma_start(second[:], offs2)
        lam_col = keep.tile([P, 1], F32, name="lam_col")
        nc.sync.dma_start(out=lam_col[:], in_=lam)
        places = lists.tile([P, SLOTS // HEAD_ROWS], U16, name="places")
        nc.sync.dma_start(places[:], offs3)
        old_sb = keep.tile([P, T], F32, name="old_sb")
        nc.sync.dma_start(out=old_sb[:], in_=old)

        placed = keep.tile([P, T], F32, name="placed")
        nc.vector.memset(placed[:], 0.0)

        codes, scales = [], []
        for j in range(2):
            grouped = keep.tile([P, Q, PACK], BF16, name="grouped%d" % j, tag="grouped", align_bytes=64)
            codes.append(keep.tile([P, Q], U32, name="codes%d" % j, align_bytes=64))
            scales.append(keep.tile([P, Q], U8, name="scales%d" % j, align_bytes=64))
            halves = (slice(0, Q // 2), slice(Q // 2, Q))
            for rows in halves:
                nc.vector.tensor_copy(
                    out=grouped[:, rows, :].rearrange("p (c i) t -> p c t i", i=RUN),
                    in_=raw[j][:, :, rows].rearrange("p t (c i) -> p c t i", i=RUN),
                )
            for rows in halves:
                nc.vector.quantize_mx(
                    out=codes[j][:, rows].bitcast(FP8X4),
                    scales=scales[j][:, rows],
                    in_=grouped[:, rows, :].rearrange("p w j -> p (w j)"),
                )

        scores = [keep.tile([P, T], F32, name="scores%d" % j) for j in range(2)]
        passes = [(j, n0, width) for j in range(2) for n0, width in PASSES]
        for k, (j, n0, width) in enumerate(passes):
            bank = psum.tile([P, width], F32, name="bank%d_%d" % (j, n0), tag="bank%d" % (k % BANKS))
            byte0 = 2 * n0
            nc.tensor.matmul_mx(
                out=bank[:],
                lhsT=codes[j][:].bitcast(FP8X4),
                lhsT_scale=scales[j][:],
                rhs=key_words[byte0 // T][:, byte0 % T : byte0 % T + 2 * width].bitcast(FP4X4),
                rhs_scale=key_scales[:, n0 : n0 + width],
                start=True,
                stop=True,
            )
            if j == 0 and n0 + width == T:
                nc.vector.tensor_copy(out=scores[j][:, n0 : n0 + width], in_=bank[:])
            else:
                nc.scalar.copy(scores[j][:, n0 : n0 + width], bank[:])
        a, b = scores

        for h in range(2):
            cols = slice(h * HALF // HEAD_ROWS, (h + 1) * HALF // HEAD_ROWS)
            from_a = keep.tile([P, 2, HALF], F32, name="from_a%d" % h, tag="pair%d" % h)
            from_b = keep.tile([P, 2, HALF], F32, name="from_b%d" % h)
            if h == 0:
                nc.vector.tensor_copy(from_a[:, 0, :], a[:].indirect(first[:, cols]))
                nc.vector.tensor_copy(from_a[:, 1, :], a[:].indirect(second[:, cols]))
                nc.vector.tensor_copy(from_b[:, 0, :], b[:].indirect(second[:, cols]))
                nc.scalar.activation(from_b[:, 1, :], b[:].indirect(first[:, cols]), COPY)
            else:
                nc.scalar.activation(from_b[:, 0, :], b[:].indirect(second[:, cols]), COPY)
                nc.scalar.activation(from_b[:, 1, :], b[:].indirect(first[:, cols]), COPY)
                nc.scalar.activation(from_a[:, 0, :], a[:].indirect(first[:, cols]), COPY)
                nc.scalar.activation(from_a[:, 1, :], a[:].indirect(second[:, cols]), COPY)
            larger = keep.tile([P, 2, HALF], F32, name="larger%d" % h, tag="pair%d" % (h + 1))
            scaled = keep.tile([P, 2, HALF], F32, name="scaled%d" % h)
            for side in range(2):
                nc.vector.tensor_tensor(larger[:, side, :], from_a[:, side, :], from_b[:, side, :], ALU.max)
            for side, sign in enumerate((1.0, -1.0)):
                nc.vector.tensor_scalar(scaled[:, side, :], larger[:, side, :], lam_col[:], sign, ALU.mult, ALU.mult)
            nc.vector.tensor_tensor(placed[:].indirect(places[:, cols]), scaled[:, 0, :], scaled[:, 1, :], ALU.add)

        pending = None
        c0 = 0
        for width in OUT_WIDTHS:
            cols = slice(c0, c0 + width)
            top = keep.tile([P, width], F32, name="top%d" % c0)
            nc.vector.tensor_tensor(top[:], placed[:, cols], old_sb[:, cols], ALU.max)
            if pending is not None:
                add_and_store(nc, keep, old_sb, out, *pending)
            pending = (top, cols)
            c0 = c0 + width
        add_and_store(nc, keep, old_sb, out, *pending)


def add_and_store(nc, keep, old_sb, out, top, cols):
    result = keep.tile([P, cols.stop - cols.start], F32, name="result%d" % cols.start)
    nc.vector.scalar_tensor_tensor(result[:], old_sb[:, cols], 0.25, top[:], ALU.mult, ALU.add)
    nc.sync.dma_start(out=out[:, cols], in_=result[:])
